import numpy as np, ml_dtypes
CORES = [24,26,29,31,48,50,53,55]
N = 8
KT, C = 1, 128
B = 1
def setup_inputs(rng):
    return {"x": rng.standard_normal((N, 128, KT * C), dtype=np.float32).astype(ml_dtypes.bfloat16)}
def setup_inputs_big(rng):
    d = setup_inputs(rng)
    for k in ("x",): d[k] = (d[k].astype(np.float32) * 1024.0).astype(d[k].dtype)
    return d
def setup_inputs_small(rng):
    d = setup_inputs(rng)
    for k in ("x",): d[k] = (d[k].astype(np.float32) * (1 / 1024.0)).astype(d[k].dtype)
    return d
def setup_inputs_apart(rng):
    d = setup_inputs(rng)
    f = (10.0 ** rng.permutation(np.linspace(-1.5, 1.5, N))).astype(np.float32).reshape(N, 1, 1)
    for k in ("x",): d[k] = (d[k].astype(np.float32) * f).astype(d[k].dtype)
    return d
def reference(x):
    X = x.astype(np.float64)
    y = np.full((N, C, (2 * B + 1) * C), np.nan)
    for r in range(N):
        for i in range(2 * B + 1):
            s = (r + i - B) % N
            if s != r: y[r][:, C * i:C * i + C] = sum(X[r][:, C * t:C * t + C].T @ X[s][:, C * t:C * t + C] for t in range(KT))
    return {"y": y.astype(ml_dtypes.bfloat16 if x.dtype != np.float64 else np.float64)}

@@ -1,0 +1,100 @@
+from concourse.bass import DstId, RemoteDMATransfer
+
+C = 128
+WIDE = 8
+NARROW = 4
+
+SCRATCH = {
+    "xs": ("sbuf", [128, C], "bfloat16"),
+    "xl": ("sbuf", [128, C], "bfloat16"),
+    "xr": ("sbuf", [128, C], "bfloat16"),
+    "pl": ("psum", [128, 512], "float32"),
+    "pr": ("psum", [128, 512], "float32"),
+    "outl": ("sbuf", [128, C], "bfloat16"),
+    "outr": ("sbuf", [128, C], "bfloat16"),
+}
+SEMAPHORES = ["ld", "sent", "al", "ar", "ml", "mr", "cl", "cr", "sl", "sr"]
+
+
+def _bits(mask):
+    return [e for e in range(mask.bit_length()) if (mask >> e) & 1]
+
+
+def _take(allowed, used, want, first):
+    free = [e for e in _bits(allowed) if e not in used]
+    free.sort(key=lambda e: (e not in first, e))
+    got = free[:min(want, len(free))]
+    assert got and 128 % len(got) == 0
+    used.update(got)
+    return sum(1 << e for e in got), len(got)
+
+
+def _plan(T, topo):
+    cores = list(T.cores)
+    n = len(cores)
+    own = {c: [] for c in cores}
+    fwd = {c: [] for c in cores}
+    arr = {}
+    for r, a in enumerate(cores):
+        for step, side, other in ((-1, "r", "l"), (1, "l", "r")):
+            s = (r + step) % n
+            b = cores[s]
+            if topo.may_write(a, b):
+                own[a].append([b, side])
+            else:
+                f = cores[(r - step) % n]
+                assert topo.chip(f) == topo.chip(a) and topo.may_write(a, f) and topo.may_write(f, b)
+                m, k = _take(topo.mask(f, b), set(), WIDE, [])
+                fwd[f].append((other, b, side, m, k))
+                arr[(s, side)] = (k, 3)
+    for a in cores:
+        warm = [e for w in fwd[a] for e in _bits(w[3])]
+        used = set()
+        todo = sorted(own[a], key=lambda w: topo.chip(w[0]) == topo.chip(a))
+        done = []
+        for b, side in todo:
+            away = topo.chip(b) != topo.chip(a)
+            m, k = _take(topo.mask(a, b), used, WIDE if away or len(todo) == 1 else NARROW, warm)
+            done.append((b, side, m, k))
+            arr[(T.rank_of(b), side)] = (k, 2 if away else 1)
+        own[a] = done
+    return own, fwd, arr
+
+
+def rank_program(g, core, T, topo):
+    rank = T.rank_of(core)
+    if rank is None:
+        return
+    own, fwd, arr = _plan(T, topo)
+    S = T.sem
+
+    g.sync.dma_start(T.xs[:], T.x[:]).then_inc(S.ld, 16)
+
+    g.wait_ge(S.ld, 16)
+    sent = 0
+    trs = []
+    for dst, side, mask, k in own[core]:
+        rid, pid, _se = topo.addr(dst)
+        trs.append(RemoteDMATransfer(dst_ids=[DstId(rid=rid, pnc=pid)], dma_engine_mask=mask,
+                                     remote_sem=S["a" + side], src=T.xs[:], dst=T["x" + side][:]))
+        sent += k
+    g.remote_dma_fused(trs, local_sem=S.sent)
+    for have, dst, side, mask, k in fwd[core]:
+        rid, pid, _se = topo.addr(dst)
+        g.wait_ge(S["a" + have], arr[(rank, have)][0])
+        g.remote_dma(T["x" + side][:], T["x" + have][:], S["a" + side], S.sent, pid, rid, mask)
+        sent += k
+
+    order = sorted(("l", "r"), key=lambda sd: arr[(rank, sd)][1])
+    g.tensor.wait_ge(S.ld, 16)
+    for q, sd in zip((g.scalar, g.sync), order):
+        col = 0 if sd == "l" else 2 * C
+        g.tensor.wait_ge(S["a" + sd], arr[(rank, sd)][0])
+        g.tensor.matmul(T["p" + sd][:, 0:C], T.xs[:], T["x" + sd][:], True, True).then_inc(S["m" + sd], 1)
+        g.vector.wait_ge(S["m" + sd], 1)
+        g.vector.tensor_copy(T["out" + sd][:], T["p" + sd][:, 0:C]).then_inc(S["c" + sd], 1)
+        q.wait_ge(S["c" + sd], 1)
+        q.dma_start(T.y[:, col:col + C], T["out" + sd][:]).then_inc(S["s" + sd], 16)
+        q.wait_ge(S["s" + sd], 16)
+
+    g.wait_ge(S.sent, sent)

@@ -1,23 +1,36 @@
 from concourse.bass import DstId, RemoteDMATransfer
 
 C = 128
+H = C // 2
 WIDE = 8
 NARROW = 4
+FEED = 4
 
 SCRATCH = {
     "xs": ("sbuf", [128, C], "bfloat16"),
     "xl": ("sbuf", [128, C], "bfloat16"),
     "xr": ("sbuf", [128, C], "bfloat16"),
+    "xd": ("dram", [2, 128, H], "bfloat16"),
+    "xp": ("dram", [128, H], "bfloat16"),
+    "xh0": ("sbuf", [128, H], "bfloat16"),
+    "xh1": ("sbuf", [128, H], "bfloat16"),
+    "z": ("sbuf", [128, 4 * C], "bfloat16"),
     "pl": ("psum", [128, 512], "float32"),
     "pr": ("psum", [128, 512], "float32"),
+    "pq": ("psum", [128, 512], "float32"),
     "outl": ("sbuf", [128, C], "bfloat16"),
     "outr": ("sbuf", [128, C], "bfloat16"),
 }
-SEMAPHORES = ["ld", "sent", "al", "ar", "ml", "mr", "cl", "cr", "sl", "sr"]
+SEMAPHORES = ["ld", "ld0", "ld1", "sent", "al", "ar", "ap", "h0", "h1", "zs", "zp", "ml", "mr", "mq", "cl", "cr",
+              "sl", "sr"]
 
 
 def _bits(mask):
     return [e for e in range(mask.bit_length()) if (mask >> e) & 1]
+
+
+def _mask(engines):
+    return sum(1 << e for e in engines)
 
 
 def _take(allowed, used, want, first):
@@ -26,29 +39,40 @@ def _take(allowed, used, want, first):
     got = free[:min(want, len(free))]
     assert got and 128 % len(got) == 0
     used.update(got)
-    return sum(1 << e for e in got), len(got)
+    return _mask(got), len(got)
 
 
 def _plan(T, topo):
     cores = list(T.cores)
     n = len(cores)
     own = {c: [] for c in cores}
+    feed = {c: [] for c in cores}
     fwd = {c: [] for c in cores}
     arr = {}
     for r, a in enumerate(cores):
-        for step, side, other in ((-1, "r", "l"), (1, "l", "r")):
+        for step, side in ((-1, "r"), (1, "l")):
             s = (r + step) % n
             b = cores[s]
             if topo.may_write(a, b):
                 own[a].append([b, side])
-            else:
-                f = cores[(r - step) % n]
-                assert topo.chip(f) == topo.chip(a) and topo.may_write(a, f) and topo.may_write(f, b)
+                continue
+            can = [f for f in cores if f not in (a, b) and topo.chip(f) == topo.chip(a)
+                   and topo.may_write(a, f) and topo.may_write(f, b)]
+            can.sort(key=lambda f: (topo.die(f) == topo.die(a), f))
+            pick = []
+            for f in can:
+                if all(topo.die(f) != topo.die(p) for p in pick):
+                    pick.append(f)
+            assert len(pick) == 2 and not feed[a]
+            eng = _bits(topo.mask(a, pick[0]) & topo.mask(a, pick[1]))[0::2][:FEED]
+            for piece, f in enumerate(pick):
+                assert not fwd[f]
+                feed[a].append((piece, f, _mask(eng), len(eng)))
                 m, k = _take(topo.mask(f, b), set(), WIDE, [])
-                fwd[f].append((other, b, side, m, k))
-                arr[(s, side)] = (k, 3)
+                fwd[f].append((piece, b, m, k, len(eng)))
+            arr[(s, side)] = (k, 3)
     for a in cores:
-        warm = [e for w in fwd[a] for e in _bits(w[3])]
+        warm = [e for w in fwd[a] + feed[a] for e in _bits(w[2])]
         used = set()
         todo = sorted(own[a], key=lambda w: topo.chip(w[0]) == topo.chip(a))
         done = []
@@ -58,43 +82,81 @@ def _plan(T, topo):
             done.append((b, side, m, k))
             arr[(T.rank_of(b), side)] = (k, 2 if away else 1)
         own[a] = done
-    return own, fwd, arr
+    return own, feed, fwd, arr
 
 
 def rank_program(g, core, T, topo):
     rank = T.rank_of(core)
     if rank is None:
         return
-    own, fwd, arr = _plan(T, topo)
+    own, feed, fwd, arr = _plan(T, topo)
     S = T.sem
+    order = sorted(("l", "r"), key=lambda sd: arr[(rank, sd)][1])
+    pieces = arr[(rank, order[1])][1] == 3
 
+    for piece, _f, _m, _k in feed[core]:
+        g.sync.dma_start(T.xd[piece], T.x[piece * H:(piece + 1) * H, :]).then_inc(S["ld%d" % piece], 16)
     g.sync.dma_start(T.xs[:], T.x[:]).then_inc(S.ld, 16)
 
-    g.wait_ge(S.ld, 16)
+    if pieces:
+        g.vector.memset(T.z[:], 0.0).then_inc(S.zs, 1)
+        g.scalar.wait_ge(S.zs, 1)
+        for a in range(2):
+            for h in range(2):
+                k = 2 * a + h
+                g.scalar.dma_start(T.z[h::2, k * C:(k + 1) * C], T.x[H * a:H * a + H, :]).then_inc(S.zp, 16)
+
     sent = 0
-    trs = []
-    for dst, side, mask, k in own[core]:
-        rid, pid, _se = topo.addr(dst)
-        trs.append(RemoteDMATransfer(dst_ids=[DstId(rid=rid, pnc=pid)], dma_engine_mask=mask,
-                                     remote_sem=S["a" + side], src=T.xs[:], dst=T["x" + side][:]))
+    for piece, f, mask, k in feed[core]:
+        rid, pid, _se = topo.addr(f)
+        g.wait_ge(S["ld%d" % piece], 16)
+        g.remote_dma(T.xp[:], T.xd[piece], S.ap, S.sent, pid, rid, mask)
         sent += k
-    g.remote_dma_fused(trs, local_sem=S.sent)
-    for have, dst, side, mask, k in fwd[core]:
+    g.wait_ge(S.ld, 16)
+    calls = [own[core]]
+    if fwd[core]:
+        away = [w for w in own[core] if topo.chip(w[0]) != topo.chip(core)]
+        calls = [c for c in (away, [w for w in own[core] if w not in away]) if c]
+    for call in calls:
+        trs = []
+        for dst, side, mask, k in call:
+            rid, pid, _se = topo.addr(dst)
+            trs.append(RemoteDMATransfer(dst_ids=[DstId(rid=rid, pnc=pid)], dma_engine_mask=mask,
+                                         remote_sem=S["a" + side], src=T.xs[:], dst=T["x" + side][:]))
+            sent += k
+        g.remote_dma_fused(trs, local_sem=S.sent)
+    for piece, dst, mask, k, kfeed in fwd[core]:
         rid, pid, _se = topo.addr(dst)
-        g.wait_ge(S["a" + have], arr[(rank, have)][0])
-        g.remote_dma(T["x" + side][:], T["x" + have][:], S["a" + side], S.sent, pid, rid, mask)
+        g.wait_ge(S.ap, kfeed)
+        g.remote_dma(T["xh%d" % piece][:], T.xp[:], S["h%d" % piece], S.sent, pid, rid, mask)
         sent += k
 
-    order = sorted(("l", "r"), key=lambda sd: arr[(rank, sd)][1])
     g.tensor.wait_ge(S.ld, 16)
     for q, sd in zip((g.scalar, g.sync), order):
         col = 0 if sd == "l" else 2 * C
-        g.tensor.wait_ge(S["a" + sd], arr[(rank, sd)][0])
-        g.tensor.matmul(T["p" + sd][:, 0:C], T.xs[:], T["x" + sd][:], True, True).then_inc(S["m" + sd], 1)
-        g.vector.wait_ge(S["m" + sd], 1)
-        g.vector.tensor_copy(T["out" + sd][:], T["p" + sd][:, 0:C]).then_inc(S["c" + sd], 1)
-        q.wait_ge(S["c" + sd], 1)
-        q.dma_start(T.y[:, col:col + C], T["out" + sd][:]).then_inc(S["s" + sd], 16)
+        k, lateness = arr[(rank, sd)]
+        out = T["out" + sd]
+        if lateness < 3:
+            g.tensor.wait_ge(S["a" + sd], k)
+            g.tensor.matmul(T["p" + sd][:, 0:C], T.xs[:], T["x" + sd][:], True, True).then_inc(S["m" + sd], 1)
+            g.vector.wait_ge(S["m" + sd], 1)
+            g.vector.tensor_copy(out[:], T["p" + sd][:, 0:C]).then_inc(S["c" + sd], 1)
+            q.wait_ge(S["c" + sd], 1)
+        else:
+            banks = (T["p" + sd], T.pq)
+            done = (S["m" + sd], S.mq)
+            g.tensor.wait_ge(S.zp, 64)
+            g.tensor.wait_ge(S.h0, k)
+            for h in range(2):
+                g.tensor.matmul(banks[h][:, 0:H], T.z[:, h * C:(h + 1) * C], T.xh0[:], True, False)
+            g.tensor.wait_ge(S.h1, k)
+            for h in range(2):
+                g.tensor.matmul(banks[h][:, 0:H], T.z[:, (2 + h) * C:(3 + h) * C], T.xh1[:], False, True).then_inc(done[h], 1)
+            for h in range(2):
+                g.vector.wait_ge(done[h], 1)
+                g.vector.tensor_copy(out[:, h * H:(h + 1) * H], banks[h][:, 0:H]).then_inc(S["c" + sd], 1)
+            q.wait_ge(S["c" + sd], 2)
+        q.dma_start(T.y[:, col:col + C], out[:]).then_inc(S["s" + sd], 16)
         q.wait_ge(S["s" + sd], 16)
 
     g.wait_ge(S.sent, sent)

from concourse.bass import DstId, RemoteDMATransfer

C = 128
H = C // 2
WIDE = 8
NARROW = 4
FEED = 4

SCRATCH = {
    "xs": ("sbuf", [128, C], "bfloat16"),
    "xl": ("sbuf", [128, C], "bfloat16"),
    "xr": ("sbuf", [128, C], "bfloat16"),
    "xd": ("dram", [2, 128, H], "bfloat16"),
    "xp": ("dram", [128, H], "bfloat16"),
    "xh0": ("sbuf", [128, H], "bfloat16"),
    "xh1": ("sbuf", [128, H], "bfloat16"),
    "z": ("sbuf", [128, 4 * C], "bfloat16"),
    "pl": ("psum", [128, 512], "float32"),
    "pr": ("psum", [128, 512], "float32"),
    "pq": ("psum", [128, 512], "float32"),
    "outl": ("sbuf", [128, C], "bfloat16"),
    "outr": ("sbuf", [128, C], "bfloat16"),
}
SEMAPHORES = ["ld", "ld0", "ld1", "sent", "al", "ar", "ap", "h0", "h1", "zs", "zp", "ml", "mr", "mq", "cl", "cr",
              "sl", "sr"]


def _bits(mask):
    return [e for e in range(mask.bit_length()) if (mask >> e) & 1]


def _mask(engines):
    return sum(1 << e for e in engines)


def _take(allowed, used, want, first):
    free = [e for e in _bits(allowed) if e not in used]
    free.sort(key=lambda e: (e not in first, e))
    got = free[:min(want, len(free))]
    assert got and 128 % len(got) == 0
    used.update(got)
    return _mask(got), len(got)


def _plan(T, topo):
    cores = list(T.cores)
    n = len(cores)
    own = {c: [] for c in cores}
    feed = {c: [] for c in cores}
    fwd = {c: [] for c in cores}
    arr = {}
    for r, a in enumerate(cores):
        for step, side in ((-1, "r"), (1, "l")):
            s = (r + step) % n
            b = cores[s]
            if topo.may_write(a, b):
                own[a].append([b, side])
                continue
            can = [f for f in cores if f not in (a, b) and topo.chip(f) == topo.chip(a)
                   and topo.may_write(a, f) and topo.may_write(f, b)]
            can.sort(key=lambda f: (topo.die(f) == topo.die(a), f))
            pick = []
            for f in can:
                if all(topo.die(f) != topo.die(p) for p in pick):
                    pick.append(f)
            assert len(pick) == 2 and not feed[a]
            eng = _bits(topo.mask(a, pick[0]) & topo.mask(a, pick[1]))[0::2][:FEED]
            for piece, f in enumerate(pick):
                assert not fwd[f]
                feed[a].append((piece, f, _mask(eng), len(eng)))
                m, k = _take(topo.mask(f, b), set(), WIDE, [])
                fwd[f].append((piece, b, m, k, len(eng)))
            arr[(s, side)] = (k, 3)
    for a in cores:
        warm = [e for w in fwd[a] + feed[a] for e in _bits(w[2])]
        used = set()
        todo = sorted(own[a], key=lambda w: topo.chip(w[0]) == topo.chip(a))
        done = []
        for b, side in todo:
            away = topo.chip(b) != topo.chip(a)
            m, k = _take(topo.mask(a, b), used, WIDE if away or len(todo) == 1 else NARROW, warm)
            done.append((b, side, m, k))
            arr[(T.rank_of(b), side)] = (k, 2 if away else 1)
        own[a] = done
    return own, feed, fwd, arr


def rank_program(g, core, T, topo):
    rank = T.rank_of(core)
    if rank is None:
        return
    own, feed, fwd, arr = _plan(T, topo)
    S = T.sem
    order = sorted(("l", "r"), key=lambda sd: arr[(rank, sd)][1])
    pieces = arr[(rank, order[1])][1] == 3

    for piece, _f, _m, _k in feed[core]:
        g.sync.dma_start(T.xd[piece], T.x[piece * H:(piece + 1) * H, :]).then_inc(S["ld%d" % piece], 16)
    g.sync.dma_start(T.xs[:], T.x[:]).then_inc(S.ld, 16)

    if pieces:
        g.vector.memset(T.z[:], 0.0).then_inc(S.zs, 1)
        g.scalar.wait_ge(S.zs, 1)
        for a in range(2):
            for h in range(2):
                k = 2 * a + h
                g.scalar.dma_start(T.z[h::2, k * C:(k + 1) * C], T.x[H * a:H * a + H, :]).then_inc(S.zp, 16)

    sent = 0
    for piece, f, mask, k in feed[core]:
        rid, pid, _se = topo.addr(f)
        g.wait_ge(S["ld%d" % piece], 16)
        g.remote_dma(T.xp[:], T.xd[piece], S.ap, S.sent, pid, rid, mask)
        sent += k
    g.wait_ge(S.ld, 16)
    calls = [own[core]]
    if fwd[core]:
        away = [w for w in own[core] if topo.chip(w[0]) != topo.chip(core)]
        calls = [c for c in (away, [w for w in own[core] if w not in away]) if c]
    for call in calls:
        trs = []
        for dst, side, mask, k in call:
            rid, pid, _se = topo.addr(dst)
            trs.append(RemoteDMATransfer(dst_ids=[DstId(rid=rid, pnc=pid)], dma_engine_mask=mask,
                                         remote_sem=S["a" + side], src=T.xs[:], dst=T["x" + side][:]))
            sent += k
        g.remote_dma_fused(trs, local_sem=S.sent)
    for piece, dst, mask, k, kfeed in fwd[core]:
        rid, pid, _se = topo.addr(dst)
        g.wait_ge(S.ap, kfeed)
        g.remote_dma(T["xh%d" % piece][:], T.xp[:], S["h%d" % piece], S.sent, pid, rid, mask)
        sent += k

    g.tensor.wait_ge(S.ld, 16)
    for q, sd in zip((g.scalar, g.sync), order):
        col = 0 if sd == "l" else 2 * C
        k, lateness = arr[(rank, sd)]
        out = T["out" + sd]
        if lateness < 3:
            g.tensor.wait_ge(S["a" + sd], k)
            g.tensor.matmul(T["p" + sd][:, 0:C], T.xs[:], T["x" + sd][:], True, True).then_inc(S["m" + sd], 1)
            g.vector.wait_ge(S["m" + sd], 1)
            g.vector.tensor_copy(out[:], T["p" + sd][:, 0:C]).then_inc(S["c" + sd], 1)
            q.wait_ge(S["c" + sd], 1)
        else:
            banks = (T["p" + sd], T.pq)
            done = (S["m" + sd], S.mq)
            g.tensor.wait_ge(S.zp, 64)
            g.tensor.wait_ge(S.h0, k)
            for h in range(2):
                g.tensor.matmul(banks[h][:, 0:H], T.z[:, h * C:(h + 1) * C], T.xh0[:], True, False)
            g.tensor.wait_ge(S.h1, k)
            for h in range(2):
                g.tensor.matmul(banks[h][:, 0:H], T.z[:, (2 + h) * C:(3 + h) * C], T.xh1[:], False, True).then_inc(done[h], 1)
            for h in range(2):
                g.vector.wait_ge(done[h], 1)
                g.vector.tensor_copy(out[:, h * H:(h + 1) * H], banks[h][:, 0:H]).then_inc(S["c" + sd], 1)
            q.wait_ge(S["c" + sd], 2)
        q.dma_start(T.y[:, col:col + C], out[:]).then_inc(S["s" + sd], 16)
        q.wait_ge(S["s" + sd], 16)

    g.wait_ge(S.sent, sent)
